import numpy as np
import ml_dtypes


def mxq(x, axis, fmt="e4m3"):
    dtype, down = {"e4m3": (ml_dtypes.float8_e4m3fn, 7), "e5m2": (ml_dtypes.float8_e5m2, 14)}[fmt]
    v = np.moveaxis(np.asarray(x, np.float32).astype(ml_dtypes.bfloat16).astype(np.float64), axis, -1)
    blocks = v.reshape(v.shape[:-1] + (-1, 32))
    amax = np.abs(blocks).max(-1, keepdims=True)
    byte = np.maximum(np.where(amax > 0, np.frexp(amax)[1] - 1 + 127, 0) - down, 1)
    scale = np.exp2(byte - 127.0)
    codes = (blocks / scale).astype(np.float32).astype(dtype).astype(np.float64)
    return np.moveaxis((codes * scale).reshape(v.shape), -1, axis)


WIDE = False


def mx_kscale(k):
    if not WIDE:
        return np.ones(k)
    levels = np.array([10, -10, 5, -5, 0])
    if k % 512:
        return np.exp2(np.random.permutation(np.resize(levels, k // 32))).repeat(32)
    a = np.empty((k // 512, 16))
    for p in range(k // 512):
        a[p, :8] = np.random.permutation(np.resize(levels, 8))
        for g in range(8):
            far = levels[np.abs(levels - a[p, g]) >= 10]
            a[p, g + 8] = far[np.random.randint(len(far))]
    return np.exp2(a.ravel()).repeat(32)


def f64(x):
    return np.asarray(x).astype(np.float64)


def striped(idx):
    return np.tile(idx.reshape(-1, 16).T, (8, 1)).astype(np.uint16)


def unstriped(offs):
    return offs[:16].T.reshape(-1).astype(np.int64)


def pack_weight(w):
    k, n = w.shape
    w = f64(np.asarray(w, np.float32).astype(ml_dtypes.bfloat16)).reshape(k // 32, 32, n)
    amax = np.abs(w).max(1)
    byte = np.clip(np.where(amax > 0, np.frexp(amax)[1] - 1 + 127 - 7, 1), 1, 254)
    scaled = (w * np.exp2(127.0 - byte)[:, None, :]).reshape(k, n).astype(np.float32)
    words = np.ascontiguousarray(scaled.reshape(k // 512, 128, 4, n).transpose(0, 1, 3, 2)).astype(ml_dtypes.float8_e4m3fn).view(np.uint8)
    return words, np.ascontiguousarray(byte.astype(np.uint8).reshape(k // 512, 16, n))


def unpack_weight(words, scales):
    g, p, n, _ = words.shape
    vals = np.ascontiguousarray(words).view(ml_dtypes.float8_e4m3fn).astype(np.float64) * np.repeat(np.exp2(scales.astype(np.float64) - 127.0), 8, axis=1)[..., None]
    return vals.transpose(0, 1, 3, 2).reshape(g * 512, n)


def sigmoid(v):
    return 1.0 / (1.0 + np.exp(-np.maximum(v, -700.0)))


K, T, S, H, V, Z, W = 512, 2048, 512, 512, 256, 512, 2048
P = 2 ** 7


def setup_inputs():
    n = np.random.standard_normal
    s = mx_kscale(K)[:, None]
    packed_xT = pack_weight(n((K, T)) * s)
    packed_eT = pack_weight(n((K, W)) * s)
    return {
        "x_words": packed_xT[0],
        "x_scales": packed_xT[1],
        "w1": (n((K, H)) / np.sqrt(K) / s).astype(np.float32),
        "w2": (n((K, H)) / np.sqrt(K) / s).astype(np.float32),
        "e_words": packed_eT[0],
        "e_scales": packed_eT[1],
        "unit": (np.random.uniform(0.6, 1.4, (K, 1)) / np.sqrt(K) / s).astype(np.float32),
        "nrm": (np.tile(np.random.uniform(0.6, 1.6, W), (P, 1))).astype(np.float32),
        "offs": striped(np.random.permutation(T)[:S]),
        "ra": striped(np.random.permutation(S)[:V]),
        "rb": striped(np.random.permutation(S)[:V]),
        "lib": striped(np.random.permutation(W)[:Z]),
    }


def reference(x_words, x_scales, w1, w2, e_words, e_scales, unit, nrm, offs, ra, rb, lib):
    xq = unpack_weight(x_words, x_scales)[:, unstriped(offs)]
    y = mxq(f64(w1), 0, "e4m3").T @ xq
    yl = mxq(f64(w2), 0, "e4m3").T @ xq
    leave = sigmoid(yl[:, unstriped(ra)])
    prod = y[:, unstriped(ra)] * (-1.0 * leave + 1.0) + 0.8 * y[:, unstriped(rb)]
    hid = f64(unit) * prod
    e_lib = unpack_weight(e_words, e_scales)[:, unstriped(lib)]
    sc = mxq(hid, 0, "e4m3").T @ e_lib
    abs_ = np.abs(sc)
    return sc / (f64(nrm)[:1][:, unstriped(lib)] + abs_ + 0.3)

@@ -1,0 +1,163 @@
+from contextlib import ExitStack
+
+import concourse.mybir as mybir
+
+K, T, S, H, V, Z = 512, 2048, 512, 512, 256, 512
+FLOPS = 2 * (2 * K * H * S) + 2 * H * V * Z
+
+F32 = mybir.dt.float32
+BF16 = mybir.dt.bfloat16
+I32 = mybir.dt.int32
+U32 = mybir.dt.uint32
+U16 = mybir.dt.uint16
+U8 = mybir.dt.uint8
+FP8X4 = mybir.dt.float8_e4m3fn_x4
+ACT = mybir.ActivationFunctionType
+ALU = mybir.AluOpType
+
+P = 128
+PACK = 4
+CH = 256
+
+
+def tile_picked_yrxnlib_tan_p_kernel(
+    tc, x_words, x_scales, w1, w2, e_words, e_scales, unit, nrm, offs, ra, rb, lib, out
+):
+    nc = tc.nc
+    with ExitStack() as ctx:
+        sb = ctx.enter_context(tc.tile_pool(name="sb", bufs=1))
+        ps = ctx.enter_context(tc.psum_pool(name="ps", bufs=1))
+
+        offs_t = sb.tile([P, S // 16], U16, name="offs_t")
+        lib_t = sb.tile([P, Z // 16], U16, name="lib_t")
+        ra_t = sb.tile([P, V // 16], U16, name="ra_t")
+        rb_t = sb.tile([P, V // 16], U16, name="rb_t")
+        xw = sb.tile([P, T], I32, name="xw")
+        ew = sb.tile([P, T], I32, name="ew")
+        xs = sb.tile([P, T], U8, name="xs")
+        es = sb.tile([P, T], U8, name="es")
+        w1_raw = sb.tile([P, PACK, H], F32, name="w1_raw")
+        w2_raw = sb.tile([P, PACK, H], F32, name="w2_raw")
+        nrm_t = sb.tile([P, T], F32, name="nrm_t")
+        unit_t = sb.tile([P, PACK], F32, name="unit_t")
+
+        nc.vector.memset(xs[:].bitcast(I32), 0)
+        nc.gpsimd.memset(es[:].bitcast(I32), 0)
+
+        nc.scalar.dma_start(unit_t[:], unit.rearrange("(p t) o -> p (t o)", t=PACK))
+        nc.sync.dma_start(offs_t[:], offs)
+        nc.sync.dma_start(xw[:], x_words[0].rearrange("p n r -> p (n r)").bitcast(I32))
+        for q in range(4):
+            nc.sync.dma_start(xs[32 * q : 32 * q + 4, :].bitcast(I32), x_scales[0, 4 * q : 4 * q + 4, :].bitcast(I32))
+        nc.sync.dma_start(w2_raw[:], w2.rearrange("(p j) c -> p j c", j=PACK))
+        nc.sync.dma_start(lib_t[:], lib)
+        for q in range(4):
+            nc.sync.dma_start(es[32 * q : 32 * q + 4, :].bitcast(I32), e_scales[0, 4 * q : 4 * q + 4, :].bitcast(I32))
+        nc.sync.dma_start(w1_raw[:], w1.rearrange("(p j) c -> p j c", j=PACK))
+        nc.sync.dma_start(ra_t[:], ra)
+        nc.sync.dma_start(rb_t[:], rb)
+        nc.sync.dma_start(ew[:], e_words[0].rearrange("p n r -> p (n r)").bitcast(I32))
+        nc.sync.dma_start(nrm_t[:], nrm)
+
+        half_unit = sb.tile([P, PACK], F32, name="half_unit")
+        nc.scalar.activation(half_unit[:], unit_t[:], ACT.Copy, scale=-0.5)
+
+        xg_s = sb.tile([P, S], U8, name="xg_s", align_bytes=64)
+        xg_w = sb.tile([P, S], U32, name="xg_w", align_bytes=64)
+        eg_s = sb.tile([P, Z], U8, name="eg_s", align_bytes=64)
+        eg_w = sb.tile([P, Z], U32, name="eg_w", align_bytes=64)
+        nc.vector.tensor_copy(xg_w[:], xw[:].bitcast(U32).indirect(offs_t[:]))
+        nc.vector.tensor_copy(xg_s[:], xs[:].indirect(offs_t[:]))
+
+        def weights(raw, name, split):
+            grouped = sb.tile([P, PACK * H], BF16, name=name + "_bf", align_bytes=64)
+            dst = grouped[:].rearrange("p (t m j) -> p m j t", t=PACK, j=PACK)
+            src = raw[:].rearrange("p j (m t) -> p m j t", t=PACK)
+            if split:
+                nc.scalar.activation(dst[:, :split], src[:, :split], ACT.Copy)
+            nc.vector.tensor_copy(dst[:, split:], src[:, split:])
+            codes = sb.tile([P, H], U32, name=name + "_codes", align_bytes=64)
+            scales = sb.tile([P, H], U8, name=name + "_scales", align_bytes=64)
+            for h in range(2):
+                nc.vector.quantize_mx(
+                    out=codes[:, 256 * h : 256 * (h + 1)].bitcast(FP8X4),
+                    scales=scales[:, 256 * h : 256 * (h + 1)],
+                    in_=grouped[:, 1024 * h : 1024 * (h + 1)],
+                )
+            return codes, scales
+
+        def first_product(codes, scales, t, bank):
+            acc = ps.tile([P, S], F32, name=f"bank{bank}", tag=f"bank{bank}")
+            cols = slice(P * t, P * (t + 1))
+            nc.tensor.matmul_mx(
+                out=acc[:], lhsT=codes[:, cols].bitcast(FP8X4), lhsT_scale=scales[:, cols],
+                rhs=xg_w[:].bitcast(FP8X4), rhs_scale=xg_s[:], start=True, stop=True,
+            )
+            return acc
+
+        w2_codes, w2_scales = weights(w2_raw, "w2", 44)
+        th = []
+        for t in range(PACK):
+            yl = first_product(w2_codes, w2_scales, t, t)
+            th_t = sb.tile([P, S], F32, name=f"th{t}")
+            nc.scalar.activation(th_t[:], yl[:], ACT.Tanh, scale=0.5)
+            th.append(th_t)
+
+        nc.vector.tensor_copy(eg_s[:], es[:].indirect(lib_t[:]))
+        w1_codes, w1_scales = weights(w1_raw, "w1", 0)
+        kept = sb.tile([P, PACK, V], F32, name="kept")
+        joined = sb.tile([P, PACK, V], F32, name="joined")
+        yh, stay = [], []
+        for t in range(PACK):
+            y = first_product(w1_codes, w1_scales, t, PACK + t)
+            yh_t = sb.tile([P, S], F32, name=f"yh{t}")
+            nc.scalar.activation(yh_t[:], y[:], ACT.Copy, scale=half_unit[:, t : t + 1])
+            yh.append(yh_t)
+        nc.vector.tensor_copy(eg_w[:], ew[:].bitcast(U32).indirect(lib_t[:]))
+        for t in range(PACK):
+            stay_t = sb.tile([P, S], F32, name=f"stay{t}")
+            nc.vector.scalar_tensor_tensor(stay_t[:], th[t][:], 1.0, yh[t][:], ALU.subtract, ALU.mult)
+            stay.append(stay_t)
+        for t in range(PACK):
+            nc.scalar.activation(joined[:, t, :], yh[t][:].indirect(rb_t[:]), ACT.Copy, scale=-1.6)
+            nc.vector.tensor_copy(kept[:, t, :], stay[t][:].indirect(ra_t[:]))
+        ng = sb.tile([P, Z], F32, name="ng")
+        nc.scalar.activation(ng[:], nrm_t[:].indirect(lib_t[:]), ACT.Copy)
+
+        hid = sb.tile([P, PACK * V], BF16, name="hid", align_bytes=64)
+        h_codes = sb.tile([P, V], U32, name="h_codes", align_bytes=64)
+        h_scales = sb.tile([P, V], U8, name="h_scales", align_bytes=64)
+        hid_v = hid[:].rearrange("p (c i t) -> p c t i", i=4, t=PACK)
+        kept_v = kept[:].rearrange("p t (c i) -> p c t i", i=4)
+        joined_v = joined[:].rearrange("p t (c i) -> p c t i", i=4)
+        for h in range(2):
+            cs = slice(32 * h, 32 * (h + 1))
+            nc.vector.tensor_tensor(hid_v[:, cs], kept_v[:, cs], joined_v[:, cs], ALU.add)
+        for h in range(2):
+            vs = slice(P * h, P * (h + 1))
+            nc.vector.quantize_mx(out=h_codes[:, vs].bitcast(FP8X4), scales=h_scales[:, vs], in_=hid[:, 512 * h : 512 * (h + 1)])
+
+        chunks = [(h, c) for h in range(2) for c in range(Z // CH)]
+        sc, den, root = [], [], []
+        for n, (h, c) in enumerate(chunks):
+            vs, es_ = slice(P * h, P * (h + 1)), slice(CH * c, CH * (c + 1))
+            acc = ps.tile([P, CH], F32, name=f"sc{n}", tag=f"bank{n}")
+            nc.tensor.matmul_mx(
+                out=acc[:], lhsT=h_codes[:, vs].bitcast(FP8X4), lhsT_scale=h_scales[:, vs],
+                rhs=eg_w[:, es_].bitcast(FP8X4), rhs_scale=eg_s[:, es_], start=True, stop=True,
+            )
+            sc.append(acc)
+        for n, (h, c) in enumerate(chunks):
+            mag = sb.tile([P, CH], F32, name=f"mag{n}")
+            nc.scalar.activation(mag[:], sc[n][:], ACT.Abs)
+            d = sb.tile([P, CH], F32, name=f"den{n}")
+            nc.vector.scalar_tensor_tensor(d[:], mag[:], 0.3, ng[:, CH * c : CH * (c + 1)], ALU.add, ALU.add)
+            den.append(d)
+        for n, (h, c) in enumerate(chunks):
+            r = sb.tile([P, CH], F32, name=f"root{n}")
+            nc.scalar.activation(r[:], den[n][:], ACT.Abs_reciprocal_sqrt)
+            m = sb.tile([P, CH], F32, name=f"m{n}")
+            nc.vector.tensor_tensor(m[:], sc[n][:], r[:], ALU.mult)
+            o = sb.tile([P, CH], F32, name=f"o{n}")
+            nc.vector.tensor_tensor(o[:], m[:], r[:], ALU.mult)
+            nc.sync.dma_start(out[P * h : P * (h + 1), CH * c : CH * (c + 1)], o[:])

@@ -1,6 +1,7 @@
 from contextlib import ExitStack
 
 import concourse.mybir as mybir
+from concourse.masks import make_identity
 
 K, T, S, H, V, Z = 512, 2048, 512, 512, 256, 512
 FLOPS = 2 * (2 * K * H * S) + 2 * H * V * Z
@@ -34,50 +35,51 @@ def tile_picked_yrxnlib_tan_p_kernel(
         rb_t = sb.tile([P, V // 16], U16, name="rb_t")
         xw = sb.tile([P, T], I32, name="xw")
         ew = sb.tile([P, T], I32, name="ew")
-        xs = sb.tile([P, T], U8, name="xs")
-        es = sb.tile([P, T], U8, name="es")
-        w1_raw = sb.tile([P, PACK, H], F32, name="w1_raw")
-        w2_raw = sb.tile([P, PACK, H], F32, name="w2_raw")
+        xs = sb.tile([P, T], U8, name="xs", tag="w1_scales", align_bytes=64)
+        es = sb.tile([P, T], U8, name="es", tag="es", align_bytes=64)
+        w1_raw = [sb.tile([P, PACK, H // 2], F32, name=f"w1_raw{c}", tag=f"w1_raw{c}") for c in range(2)]
+        w2_raw = [sb.tile([P, PACK, H // 2], F32, name=f"w2_raw{c}", tag=f"w2_raw{c}", align_bytes=64) for c in range(2)]
         nrm_t = sb.tile([P, T], F32, name="nrm_t")
         unit_t = sb.tile([P, PACK], F32, name="unit_t")
 
-        nc.vector.memset(xs[:].bitcast(I32), 0)
-        nc.gpsimd.memset(es[:].bitcast(I32), 0)
+        nc.gpsimd.memset(xs[:].bitcast(I32), 0)
+        nc.vector.memset(es[:].bitcast(I32), 0)
+        nc.vector.memset(nrm_t[:], 0.0)
 
         nc.scalar.dma_start(unit_t[:], unit.rearrange("(p t) o -> p (t o)", t=PACK))
+        nc.scalar.dma_start(nrm_t[0:1, :], nrm[0:1, :])
+        ident = sb.tile([P, P], F32, name="ident")
+        make_identity(nc, ident[:])
+        for q in range(4):
+            nc.gpsimd.dma_start(es[32 * q : 32 * q + 4, :].bitcast(I32), e_scales[0, 4 * q : 4 * q + 4, :].bitcast(I32))
         nc.sync.dma_start(offs_t[:], offs)
-        nc.sync.dma_start(xw[:], x_words[0].rearrange("p n r -> p (n r)").bitcast(I32))
+        nc.sync.dma_start(lib_t[:], lib)
+        for c in range(2):
+            nc.sync.dma_start(w1_raw[c][:], w1.rearrange("(p j) c -> p j c", j=PACK)[:, :, 256 * c : 256 * (c + 1)])
         for q in range(4):
             nc.sync.dma_start(xs[32 * q : 32 * q + 4, :].bitcast(I32), x_scales[0, 4 * q : 4 * q + 4, :].bitcast(I32))
-        nc.sync.dma_start(w2_raw[:], w2.rearrange("(p j) c -> p j c", j=PACK))
-        nc.sync.dma_start(lib_t[:], lib)
-        for q in range(4):
-            nc.sync.dma_start(es[32 * q : 32 * q + 4, :].bitcast(I32), e_scales[0, 4 * q : 4 * q + 4, :].bitcast(I32))
-        nc.sync.dma_start(w1_raw[:], w1.rearrange("(p j) c -> p j c", j=PACK))
-        nc.sync.dma_start(ra_t[:], ra)
+        nc.sync.dma_start(xw[:], x_words[0].rearrange("p n r -> p (n r)").bitcast(I32))
         nc.sync.dma_start(rb_t[:], rb)
+        for c in range(2):
+            nc.sync.dma_start(w2_raw[c][:], w2.rearrange("(p j) c -> p j c", j=PACK)[:, :, 256 * c : 256 * (c + 1)])
+        nc.sync.dma_start(ra_t[:], ra)
         nc.sync.dma_start(ew[:], e_words[0].rearrange("p n r -> p (n r)").bitcast(I32))
-        nc.sync.dma_start(nrm_t[:], nrm)
 
-        half_unit = sb.tile([P, PACK], F32, name="half_unit")
-        nc.scalar.activation(half_unit[:], unit_t[:], ACT.Copy, scale=-0.5)
 
+        gain = sb.tile([P, PACK], F32, name="gain")
+        nc.scalar.activation(gain[:], unit_t[:], ACT.Copy, scale=0.8)
         xg_s = sb.tile([P, S], U8, name="xg_s", align_bytes=64)
-        xg_w = sb.tile([P, S], U32, name="xg_w", align_bytes=64)
-        eg_s = sb.tile([P, Z], U8, name="eg_s", align_bytes=64)
-        eg_w = sb.tile([P, Z], U32, name="eg_w", align_bytes=64)
-        nc.vector.tensor_copy(xg_w[:], xw[:].bitcast(U32).indirect(offs_t[:]))
-        nc.vector.tensor_copy(xg_s[:], xs[:].indirect(offs_t[:]))
 
-        def weights(raw, name, split):
-            grouped = sb.tile([P, PACK * H], BF16, name=name + "_bf", align_bytes=64)
-            dst = grouped[:].rearrange("p (t m j) -> p m j t", t=PACK, j=PACK)
-            src = raw[:].rearrange("p j (m t) -> p m j t", t=PACK)
-            if split:
-                nc.scalar.activation(dst[:, :split], src[:, :split], ACT.Copy)
-            nc.vector.tensor_copy(dst[:, split:], src[:, split:])
+        def dealt(name):
+            grouped = sb.tile([P, PACK * H], BF16, name=name + "_bf", tag=name + "_bf", align_bytes=64)
+            return grouped, grouped[:].rearrange("p (t m j) -> p m j t", t=PACK, j=PACK)
+
+        def by_line(raw):
+            return raw[:].rearrange("p j (m t) -> p m j t", t=PACK)
+
+        def quantised(grouped, name):
             codes = sb.tile([P, H], U32, name=name + "_codes", align_bytes=64)
-            scales = sb.tile([P, H], U8, name=name + "_scales", align_bytes=64)
+            scales = sb.tile([P, H], U8, name=name + "_scales", tag=name + "_scales", align_bytes=64)
             for h in range(2):
                 nc.vector.quantize_mx(
                     out=codes[:, 256 * h : 256 * (h + 1)].bitcast(FP8X4),
@@ -87,7 +89,7 @@ def tile_picked_yrxnlib_tan_p_kernel(
             return codes, scales
 
         def first_product(codes, scales, t, bank):
-            acc = ps.tile([P, S], F32, name=f"bank{bank}", tag=f"bank{bank}")
+            acc = ps.tile([P, S], F32, name=f"acc{bank}", tag=f"bank{bank}")
             cols = slice(P * t, P * (t + 1))
             nc.tensor.matmul_mx(
                 out=acc[:], lhsT=codes[:, cols].bitcast(FP8X4), lhsT_scale=scales[:, cols],
@@ -95,34 +97,57 @@ def tile_picked_yrxnlib_tan_p_kernel(
             )
             return acc
 
-        w2_codes, w2_scales = weights(w2_raw, "w2", 44)
+        w1_bf, w1_dst = dealt("w1")
+        for c in range(2):
+            nc.scalar.activation(w1_dst[:, 64 * c : 64 * (c + 1)], by_line(w1_raw[c]), ACT.Copy)
+        n_row = sb.tile([P, Z], F32, name="n_row", tag="w1_raw1")
+        nc.scalar.activation(n_row[:], nrm_t[:].indirect(lib_t[:]), ACT.Copy, bias=0.3)
+        nc.vector.tensor_copy(xg_s[:], xs[:].indirect(offs_t[:]))
+        w1_codes, w1_scales = quantised(w1_bf, "w1")
+        xg_w = sb.tile([P, S], U32, name="xg_w", tag="w1_bf", align_bytes=64)
+        nc.vector.tensor_copy(xg_w[:], xw[:].bitcast(U32).indirect(offs_t[:]))
+        yh = []
+        for t in range(PACK):
+            y = first_product(w1_codes, w1_scales, t, t)
+            yh_t = sb.tile([P, S], F32, name=f"yh{t}")
+            nc.scalar.activation(yh_t[:], y[:], ACT.Copy, scale=gain[:, t : t + 1])
+            yh.append(yh_t)
+
+        w2_bf, w2_dst = dealt("w2")
+        for c in range(2):
+            nc.vector.tensor_copy(w2_dst[:, 64 * c : 64 * (c + 1)], by_line(w2_raw[c]))
+        w2_codes, w2_scales = quantised(w2_bf, "w2")
         th = []
         for t in range(PACK):
-            yl = first_product(w2_codes, w2_scales, t, t)
-            th_t = sb.tile([P, S], F32, name=f"th{t}")
+            yl = first_product(w2_codes, w2_scales, t, PACK + t)
+            th_t = sb.tile([P, S], F32, name=f"th{t}", tag=f"th{t}", align_bytes=64)
             nc.scalar.activation(th_t[:], yl[:], ACT.Tanh, scale=0.5)
             th.append(th_t)
 
+        turned = ps.tile([P, PACK, P], F32, name="turned", tag="bank4")
+        for c in range(Z // P):
+            nc.tensor.transpose(turned[:, c, :], n_row[:, P * c : P * (c + 1)], ident[:])
+        n_col = sb.tile([P, Z // P], F32, name="n_col")
+        nc.scalar.activation(n_col[:], turned[:, :, 0], ACT.Copy)
+        ng = ps.tile([P, Z], F32, name="ng", tag="bank5")
+        for c in range(Z // P):
+            nc.tensor.transpose(ng[:, P * c : P * (c + 1)], n_col[:, c : c + 1].to_broadcast([P, P]), ident[:])
+        kept = sb.tile([P, PACK, V], F32, name="kept", tag="th1", align_bytes=64)
+        joined = sb.tile([P, PACK, V], F32, name="joined", tag="w2_bf", align_bytes=64)
+        for t in range(PACK - 1):
+            nc.vector.tensor_copy(joined[:, t, :], yh[t][:].indirect(rb_t[:]))
+        eg_s = sb.tile([P, Z], U8, name="eg_s", tag="w2_raw1", align_bytes=64)
         nc.vector.tensor_copy(eg_s[:], es[:].indirect(lib_t[:]))
-        w1_codes, w1_scales = weights(w1_raw, "w1", 0)
-        kept = sb.tile([P, PACK, V], F32, name="kept")
-        joined = sb.tile([P, PACK, V], F32, name="joined")
-        yh, stay = [], []
+        stay = []
         for t in range(PACK):
-            y = first_product(w1_codes, w1_scales, t, PACK + t)
-            yh_t = sb.tile([P, S], F32, name=f"yh{t}")
-            nc.scalar.activation(yh_t[:], y[:], ACT.Copy, scale=half_unit[:, t : t + 1])
-            yh.append(yh_t)
-        nc.vector.tensor_copy(eg_w[:], ew[:].bitcast(U32).indirect(lib_t[:]))
-        for t in range(PACK):
-            stay_t = sb.tile([P, S], F32, name=f"stay{t}")
+            stay_t = sb.tile([P, S], F32, name=f"stay{t}", tag=f"stay{t}")
             nc.vector.scalar_tensor_tensor(stay_t[:], th[t][:], 1.0, yh[t][:], ALU.subtract, ALU.mult)
             stay.append(stay_t)
+        nc.scalar.activation(joined[:, PACK - 1, :], yh[PACK - 1][:].indirect(rb_t[:]), ACT.Copy)
         for t in range(PACK):
-            nc.scalar.activation(joined[:, t, :], yh[t][:].indirect(rb_t[:]), ACT.Copy, scale=-1.6)
-            nc.vector.tensor_copy(kept[:, t, :], stay[t][:].indirect(ra_t[:]))
-        ng = sb.tile([P, Z], F32, name="ng")
-        nc.scalar.activation(ng[:], nrm_t[:].indirect(lib_t[:]), ACT.Copy)
+            nc.scalar.activation(kept[:, t, :], stay[t][:].indirect(ra_t[:]), ACT.Copy, scale=-0.625)
+        eg_w = sb.tile([P, Z], U32, name="eg_w", tag="th3", align_bytes=64)
+        nc.vector.tensor_copy(eg_w[:], ew[:].bitcast(U32).indirect(lib_t[:]))
 
         hid = sb.tile([P, PACK * V], BF16, name="hid", align_bytes=64)
         h_codes = sb.tile([P, V], U32, name="h_codes", align_bytes=64)
@@ -133,7 +158,6 @@ def tile_picked_yrxnlib_tan_p_kernel(
         for h in range(2):
             cs = slice(32 * h, 32 * (h + 1))
             nc.vector.tensor_tensor(hid_v[:, cs], kept_v[:, cs], joined_v[:, cs], ALU.add)
-        for h in range(2):
             vs = slice(P * h, P * (h + 1))
             nc.vector.quantize_mx(out=h_codes[:, vs].bitcast(FP8X4), scales=h_scales[:, vs], in_=hid[:, 512 * h : 512 * (h + 1)])
 
@@ -148,16 +172,19 @@ def tile_picked_yrxnlib_tan_p_kernel(
             )
             sc.append(acc)
         for n, (h, c) in enumerate(chunks):
+            cols = slice(CH * c, CH * (c + 1))
             mag = sb.tile([P, CH], F32, name=f"mag{n}")
             nc.scalar.activation(mag[:], sc[n][:], ACT.Abs)
             d = sb.tile([P, CH], F32, name=f"den{n}")
-            nc.vector.scalar_tensor_tensor(d[:], mag[:], 0.3, ng[:, CH * c : CH * (c + 1)], ALU.add, ALU.add)
-            den.append(d)
-        for n, (h, c) in enumerate(chunks):
+            nc.vector.tensor_tensor(d[:], ng[:, cols], mag[:], ALU.add)
             r = sb.tile([P, CH], F32, name=f"root{n}")
-            nc.scalar.activation(r[:], den[n][:], ACT.Abs_reciprocal_sqrt)
+            nc.scalar.activation(r[:], d[:], ACT.Abs_reciprocal_sqrt)
             m = sb.tile([P, CH], F32, name=f"m{n}")
-            nc.vector.tensor_tensor(m[:], sc[n][:], r[:], ALU.mult)
             o = sb.tile([P, CH], F32, name=f"o{n}")
-            nc.vector.tensor_tensor(o[:], m[:], r[:], ALU.mult)
-            nc.sync.dma_start(out[P * h : P * (h + 1), CH * c : CH * (c + 1)], o[:])
+            if n < 2:
+                nc.scalar.activation(m[:], r[:], ACT.Square)
+                nc.vector.tensor_tensor(o[:], sc[n][:], m[:], ALU.mult)
+            else:
+                nc.vector.tensor_tensor(m[:], sc[n][:], r[:], ALU.mult)
+                nc.vector.tensor_tensor(o[:], m[:], r[:], ALU.mult)
+            nc.sync.dma_start(out[P * h : P * (h + 1), cols], o[:])

@@ -149,6 +149,8 @@ def tile_picked_yrxnlib_tan_p_kernel(
         eg_w = sb.tile([P, Z], U32, name="eg_w", tag="th3", align_bytes=64)
         nc.vector.tensor_copy(eg_w[:], ew[:].bitcast(U32).indirect(lib_t[:]))
 
+        warm = sb.tile([P, 1], F32, name="warm")
+        nc.scalar.activation(warm[:], kept[:, PACK - 1, 0:1], ACT.Abs_reciprocal_sqrt)
         hid = sb.tile([P, PACK * V], BF16, name="hid", align_bytes=64)
         h_codes = sb.tile([P, V], U32, name="h_codes", align_bytes=64)
         h_scales = sb.tile([P, V], U8, name="h_scales", align_bytes=64)

@@ -19,6 +19,9 @@ ALU = mybir.AluOpType
 P = 128
 PACK = 4
 CH = 256
+SPLIT = 20
+LAST = PACK - 1
+TOP = P - 16
 
 
 def tile_picked_yrxnlib_tan_p_kernel(
@@ -35,44 +38,60 @@ def tile_picked_yrxnlib_tan_p_kernel(
         rb_t = sb.tile([P, V // 16], U16, name="rb_t")
         xw = sb.tile([P, T], I32, name="xw")
         ew = sb.tile([P, T], I32, name="ew")
-        xs = sb.tile([P, T], U8, name="xs", tag="w1_scales", align_bytes=64)
-        es = sb.tile([P, T], U8, name="es", tag="es", align_bytes=64)
+        xs = sb.tile([P, T], U8, name="xs")
+        es = sb.tile([P, T], U8, name="es")
+        eg_s = sb.tile([P, Z], U8, name="eg_s", align_bytes=64)
         w1_raw = [sb.tile([P, PACK, H // 2], F32, name=f"w1_raw{c}", tag=f"w1_raw{c}") for c in range(2)]
         w2_raw = [sb.tile([P, PACK, H // 2], F32, name=f"w2_raw{c}", tag=f"w2_raw{c}", align_bytes=64) for c in range(2)]
         nrm_t = sb.tile([P, T], F32, name="nrm_t")
         unit_t = sb.tile([P, PACK], F32, name="unit_t")
 
         nc.gpsimd.memset(xs[:].bitcast(I32), 0)
-        nc.vector.memset(es[:].bitcast(I32), 0)
-        nc.vector.memset(nrm_t[:], 0.0)
+        nc.vector.memset(es[:TOP, :].bitcast(I32), 0)
+        nc.vector.memset(nrm_t[: P - 1, :], 0.0)
+        nc.vector.memset(eg_s[:].bitcast(I32), 0)
 
-        nc.scalar.dma_start(unit_t[:], unit.rearrange("(p t) o -> p (t o)", t=PACK))
-        nc.scalar.dma_start(nrm_t[0:1, :], nrm[0:1, :])
+        nc.scalar.dma_start(es[TOP:, :].bitcast(I32), e_scales[0].bitcast(I32))
+        nc.scalar.dma_start(nrm_t[P - 1 :, :], nrm[0:1, :])
+        nc.gpsimd.dma_start(unit_t[:], unit.rearrange("(p t) o -> p (t o)", t=PACK))
         ident = sb.tile([P, P], F32, name="ident")
         make_identity(nc, ident[:])
-        for q in range(4):
-            nc.gpsimd.dma_start(es[32 * q : 32 * q + 4, :].bitcast(I32), e_scales[0, 4 * q : 4 * q + 4, :].bitcast(I32))
         nc.sync.dma_start(offs_t[:], offs)
         nc.sync.dma_start(lib_t[:], lib)
-        for c in range(2):
-            nc.sync.dma_start(w1_raw[c][:], w1.rearrange("(p j) c -> p j c", j=PACK)[:, :, 256 * c : 256 * (c + 1)])
+        nc.sync.dma_start(xw[:], x_words[0].rearrange("p n r -> p (n r)").bitcast(I32))
         for q in range(4):
             nc.sync.dma_start(xs[32 * q : 32 * q + 4, :].bitcast(I32), x_scales[0, 4 * q : 4 * q + 4, :].bitcast(I32))
-        nc.sync.dma_start(xw[:], x_words[0].rearrange("p n r -> p (n r)").bitcast(I32))
+        for c in range(2):
+            nc.sync.dma_start(w1_raw[c][:], w1.rearrange("(p j) c -> p j c", j=PACK)[:, :, 256 * c : 256 * (c + 1)])
         nc.sync.dma_start(rb_t[:], rb)
         for c in range(2):
             nc.sync.dma_start(w2_raw[c][:], w2.rearrange("(p j) c -> p j c", j=PACK)[:, :, 256 * c : 256 * (c + 1)])
         nc.sync.dma_start(ra_t[:], ra)
         nc.sync.dma_start(ew[:], e_words[0].rearrange("p n r -> p (n r)").bitcast(I32))
 
+        eg_apart = sb.tile([P, Z], U8, name="eg_apart")
+        nc.vector.tensor_copy(eg_apart[:], es[:].indirect(lib_t[:]))
+        for q in range(4):
+            nc.sync.dma_start(eg_s[32 * q : 32 * q + 4, :].bitcast(I32), eg_apart[TOP + 4 * q : TOP + 4 * q + 4, :].bitcast(I32))
+
+        n_row = sb.tile([P, Z], F32, name="n_row")
+        nc.scalar.activation(n_row[:], nrm_t[:].indirect(lib_t[:]), ACT.Copy, bias=0.3)
+        turned = ps.tile([P, PACK, P], F32, name="turned", tag="bank4")
+        for c in range(Z // P):
+            nc.tensor.transpose(turned[:, c, :], n_row[:, P * c : P * (c + 1)], ident[:])
+        n_col = sb.tile([P, Z // P], F32, name="n_col")
+        nc.scalar.activation(n_col[:], turned[:, :, P - 1], ACT.Copy)
+        ng = ps.tile([P, Z], F32, name="ng", tag="bank7")
+        for c in range(Z // P):
+            nc.tensor.transpose(ng[:, P * c : P * (c + 1)], n_col[:, c : c + 1].to_broadcast([P, P]), ident[:])
 
         gain = sb.tile([P, PACK], F32, name="gain")
-        nc.scalar.activation(gain[:], unit_t[:], ACT.Copy, scale=0.8)
+        nc.gpsimd.tensor_scalar(gain[:, :LAST], unit_t[:, :LAST], 0.8, 0.0, ALU.mult, ALU.add)
+        nc.gpsimd.tensor_scalar(gain[:, LAST:], unit_t[:, LAST:], 0.5, 0.0, ALU.mult, ALU.add)
         xg_s = sb.tile([P, S], U8, name="xg_s", align_bytes=64)
 
-        def dealt(name):
-            grouped = sb.tile([P, PACK * H], BF16, name=name + "_bf", tag=name + "_bf", align_bytes=64)
-            return grouped, grouped[:].rearrange("p (t m j) -> p m j t", t=PACK, j=PACK)
+        def dealt(grouped):
+            return grouped.rearrange("p (t m j) -> p m j t", t=PACK, j=PACK)
 
         def by_line(raw):
             return raw[:].rearrange("p j (m t) -> p m j t", t=PACK)
@@ -89,7 +108,7 @@ def tile_picked_yrxnlib_tan_p_kernel(
             return codes, scales
 
         def first_product(codes, scales, t, bank):
-            acc = ps.tile([P, S], F32, name=f"acc{bank}", tag=f"bank{bank}")
+            acc = ps.tile([P, S], F32, name=f"acc{bank}_{t}", tag=f"bank{bank}")
             cols = slice(P * t, P * (t + 1))
             nc.tensor.matmul_mx(
                 out=acc[:], lhsT=codes[:, cols].bitcast(FP8X4), lhsT_scale=scales[:, cols],
@@ -97,15 +116,16 @@ def tile_picked_yrxnlib_tan_p_kernel(
             )
             return acc
 
-        w1_bf, w1_dst = dealt("w1")
-        for c in range(2):
-            nc.scalar.activation(w1_dst[:, 64 * c : 64 * (c + 1)], by_line(w1_raw[c]), ACT.Copy)
-        n_row = sb.tile([P, Z], F32, name="n_row", tag="w1_raw1")
-        nc.scalar.activation(n_row[:], nrm_t[:].indirect(lib_t[:]), ACT.Copy, bias=0.3)
-        nc.vector.tensor_copy(xg_s[:], xs[:].indirect(offs_t[:]))
-        w1_codes, w1_scales = quantised(w1_bf, "w1")
-        xg_w = sb.tile([P, S], U32, name="xg_w", tag="w1_bf", align_bytes=64)
+        w1_tile = sb.tile([P, PACK * H], BF16, name="w1_bf", align_bytes=64)
+        w1_bf = w1_tile[:]
+        w1_dst = dealt(w1_bf)
+        xg_w = sb.tile([P, S], U32, name="xg_w", align_bytes=64)
         nc.vector.tensor_copy(xg_w[:], xw[:].bitcast(U32).indirect(offs_t[:]))
+        nc.vector.tensor_copy(xg_s[:], xs[:].indirect(offs_t[:]))
+        nc.scalar.activation(w1_dst[:, :64], by_line(w1_raw[0]), ACT.Copy)
+        nc.scalar.activation(w1_dst[:, 64 : 64 + SPLIT], by_line(w1_raw[1])[:, :SPLIT], ACT.Copy)
+        nc.vector.tensor_copy(w1_dst[:, 64 + SPLIT :], by_line(w1_raw[1])[:, SPLIT:])
+        w1_codes, w1_scales = quantised(w1_bf, "w1")
         yh = []
         for t in range(PACK):
             y = first_product(w1_codes, w1_scales, t, t)
@@ -113,44 +133,37 @@ def tile_picked_yrxnlib_tan_p_kernel(
             nc.scalar.activation(yh_t[:], y[:], ACT.Copy, scale=gain[:, t : t + 1])
             yh.append(yh_t)
 
-        w2_bf, w2_dst = dealt("w2")
+        w2_tile = sb.tile([P, PACK * H], BF16, name="w2_bf", tag="w2_bf", align_bytes=64)
+        w2_bf = w2_tile[:]
+        w2_dst = dealt(w2_bf)
         for c in range(2):
             nc.vector.tensor_copy(w2_dst[:, 64 * c : 64 * (c + 1)], by_line(w2_raw[c]))
         w2_codes, w2_scales = quantised(w2_bf, "w2")
         th = []
         for t in range(PACK):
-            yl = first_product(w2_codes, w2_scales, t, PACK + t)
+            yl = first_product(w2_codes, w2_scales, t, (PACK + t) % 7)
             th_t = sb.tile([P, S], F32, name=f"th{t}", tag=f"th{t}", align_bytes=64)
-            nc.scalar.activation(th_t[:], yl[:], ACT.Tanh, scale=0.5)
+            nc.scalar.activation(th_t[:], yl[:], ACT.Tanh, scale=-0.5)
             th.append(th_t)
 
-        turned = ps.tile([P, PACK, P], F32, name="turned", tag="bank4")
-        for c in range(Z // P):
-            nc.tensor.transpose(turned[:, c, :], n_row[:, P * c : P * (c + 1)], ident[:])
-        n_col = sb.tile([P, Z // P], F32, name="n_col")
-        nc.scalar.activation(n_col[:], turned[:, :, 0], ACT.Copy)
-        ng = ps.tile([P, Z], F32, name="ng", tag="bank5")
-        for c in range(Z // P):
-            nc.tensor.transpose(ng[:, P * c : P * (c + 1)], n_col[:, c : c + 1].to_broadcast([P, P]), ident[:])
         kept = sb.tile([P, PACK, V], F32, name="kept", tag="th1", align_bytes=64)
         joined = sb.tile([P, PACK, V], F32, name="joined", tag="w2_bf", align_bytes=64)
-        for t in range(PACK - 1):
+        for t in range(LAST):
             nc.vector.tensor_copy(joined[:, t, :], yh[t][:].indirect(rb_t[:]))
-        eg_s = sb.tile([P, Z], U8, name="eg_s", tag="w2_raw1", align_bytes=64)
-        nc.vector.tensor_copy(eg_s[:], es[:].indirect(lib_t[:]))
+        nc.scalar.activation(joined[:, LAST, :], yh[LAST][:].indirect(rb_t[:]), ACT.Copy, scale=1.6)
         stay = []
         for t in range(PACK):
             stay_t = sb.tile([P, S], F32, name=f"stay{t}", tag=f"stay{t}")
-            nc.vector.scalar_tensor_tensor(stay_t[:], th[t][:], 1.0, yh[t][:], ALU.subtract, ALU.mult)
+            nc.vector.scalar_tensor_tensor(stay_t[:], th[t][:], 1.0, yh[t][:], ALU.add, ALU.mult)
             stay.append(stay_t)
-        nc.scalar.activation(joined[:, PACK - 1, :], yh[PACK - 1][:].indirect(rb_t[:]), ACT.Copy)
-        for t in range(PACK):
-            nc.scalar.activation(kept[:, t, :], stay[t][:].indirect(ra_t[:]), ACT.Copy, scale=-0.625)
+        for t in range(LAST):
+            nc.scalar.activation(kept[:, t, :], stay[t][:].indirect(ra_t[:]), ACT.Copy, scale=0.625)
+        nc.vector.tensor_copy(kept[:, LAST, :], stay[LAST][:].indirect(ra_t[:]))
         eg_w = sb.tile([P, Z], U32, name="eg_w", tag="th3", align_bytes=64)
         nc.vector.tensor_copy(eg_w[:], ew[:].bitcast(U32).indirect(lib_t[:]))
 
         warm = sb.tile([P, 1], F32, name="warm")
-        nc.scalar.activation(warm[:], kept[:, PACK - 1, 0:1], ACT.Abs_reciprocal_sqrt)
+        nc.scalar.activation(warm[:], kept[:, LAST - 1, 0:1], ACT.Abs_reciprocal_sqrt)
         hid = sb.tile([P, PACK * V], BF16, name="hid", align_bytes=64)
         h_codes = sb.tile([P, V], U32, name="h_codes", align_bytes=64)
         h_scales = sb.tile([P, V], U8, name="h_scales", align_bytes=64)
@@ -167,7 +180,7 @@ def tile_picked_yrxnlib_tan_p_kernel(
         sc, den, root = [], [], []
         for n, (h, c) in enumerate(chunks):
             vs, es_ = slice(P * h, P * (h + 1)), slice(CH * c, CH * (c + 1))
-            acc = ps.tile([P, CH], F32, name=f"sc{n}", tag=f"bank{n}")
+            acc = ps.tile([P, CH], F32, name=f"sc{n}", tag=f"bank{n + 1}")
             nc.tensor.matmul_mx(
                 out=acc[:], lhsT=h_codes[:, vs].bitcast(FP8X4), lhsT_scale=h_scales[:, vs],
                 rhs=eg_w[:, es_].bitcast(FP8X4), rhs_scale=eg_s[:, es_], start=True, stop=True,

@@ -158,26 +158,27 @@ def tile_picked_yrxnlib_tan_p_kernel(
             stay.append(stay_t)
         for t in range(LAST):
             nc.scalar.activation(kept[:, t, :], stay[t][:].indirect(ra_t[:]), ACT.Copy, scale=0.625)
-        nc.vector.tensor_copy(kept[:, LAST, :], stay[LAST][:].indirect(ra_t[:]))
+        nc.scalar.activation(kept[:, LAST, :P], stay[LAST][:].indirect(ra_t[:, : P // 16]), ACT.Copy)
+        nc.vector.tensor_copy(kept[:, LAST, P:], stay[LAST][:].indirect(ra_t[:, P // 16 :]))
         eg_w = sb.tile([P, Z], U32, name="eg_w", tag="th3", align_bytes=64)
         nc.vector.tensor_copy(eg_w[:], ew[:].bitcast(U32).indirect(lib_t[:]))
 
         warm = sb.tile([P, 1], F32, name="warm")
-        nc.scalar.activation(warm[:], kept[:, LAST - 1, 0:1], ACT.Abs_reciprocal_sqrt)
-        hid = sb.tile([P, PACK * V], BF16, name="hid", align_bytes=64)
+        nc.scalar.activation(warm[:], kept[:, LAST, 0:1], ACT.Abs_reciprocal_sqrt)
         h_codes = sb.tile([P, V], U32, name="h_codes", align_bytes=64)
         h_scales = sb.tile([P, V], U8, name="h_scales", align_bytes=64)
-        hid_v = hid[:].rearrange("p (c i t) -> p c t i", i=4, t=PACK)
         kept_v = kept[:].rearrange("p t (c i) -> p c t i", i=4)
         joined_v = joined[:].rearrange("p t (c i) -> p c t i", i=4)
         for h in range(2):
             cs = slice(32 * h, 32 * (h + 1))
-            nc.vector.tensor_tensor(hid_v[:, cs], kept_v[:, cs], joined_v[:, cs], ALU.add)
+            hid = sb.tile([P, PACK * P], BF16, name=f"hid{h}", align_bytes=64)
+            hid_v = hid[:].rearrange("p (c i t) -> p c t i", i=4, t=PACK)
+            nc.vector.tensor_tensor(hid_v, kept_v[:, cs], joined_v[:, cs], ALU.add)
             vs = slice(P * h, P * (h + 1))
-            nc.vector.quantize_mx(out=h_codes[:, vs].bitcast(FP8X4), scales=h_scales[:, vs], in_=hid[:, 512 * h : 512 * (h + 1)])
+            nc.vector.quantize_mx(out=h_codes[:, vs].bitcast(FP8X4), scales=h_scales[:, vs], in_=hid[:])
 
         chunks = [(h, c) for h in range(2) for c in range(Z // CH)]
-        sc, den, root = [], [], []
+        sc = []
         for n, (h, c) in enumerate(chunks):
             vs, es_ = slice(P * h, P * (h + 1)), slice(CH * c, CH * (c + 1))
             acc = ps.tile([P, CH], F32, name=f"sc{n}", tag=f"bank{n + 1}")
@@ -186,20 +187,30 @@ def tile_picked_yrxnlib_tan_p_kernel(
                 rhs=eg_w[:, es_].bitcast(FP8X4), rhs_scale=eg_s[:, es_], start=True, stop=True,
             )
             sc.append(acc)
-        for n, (h, c) in enumerate(chunks):
+        work = {
+            name: [sb.tile([P, CH], F32, name=f"{name}{n}") for n in range(len(chunks))]
+            for name in ("mag", "den", "root", "part", "res")
+        }
+
+        def stage(k, n):
+            h, c = chunks[n]
             cols = slice(CH * c, CH * (c + 1))
-            mag = sb.tile([P, CH], F32, name=f"mag{n}")
-            nc.scalar.activation(mag[:], sc[n][:], ACT.Abs)
-            d = sb.tile([P, CH], F32, name=f"den{n}")
-            nc.vector.tensor_tensor(d[:], ng[:, cols], mag[:], ALU.add)
-            r = sb.tile([P, CH], F32, name=f"root{n}")
-            nc.scalar.activation(r[:], d[:], ACT.Abs_reciprocal_sqrt)
-            m = sb.tile([P, CH], F32, name=f"m{n}")
-            o = sb.tile([P, CH], F32, name=f"o{n}")
-            if n < 2:
-                nc.scalar.activation(m[:], r[:], ACT.Square)
-                nc.vector.tensor_tensor(o[:], sc[n][:], m[:], ALU.mult)
+            mag, den, root, part, res = (work[name][n] for name in ("mag", "den", "root", "part", "res"))
+            if k == 0:
+                nc.scalar.activation(mag[:], sc[n][:], ACT.Abs)
+            elif k == 1:
+                nc.vector.tensor_tensor(den[:], ng[:, cols], mag[:], ALU.add)
+            elif k == 2:
+                nc.scalar.activation(root[:], den[:], ACT.Abs_reciprocal_sqrt)
+            elif k == 3 and n >= 2:
+                nc.scalar.activation(part[:], root[:], ACT.Square)
+            elif k == 3:
+                nc.vector.tensor_tensor(part[:], sc[n][:], root[:], ALU.mult)
             else:
-                nc.vector.tensor_tensor(m[:], sc[n][:], r[:], ALU.mult)
-                nc.vector.tensor_tensor(o[:], m[:], r[:], ALU.mult)
-            nc.sync.dma_start(out[P * h : P * (h + 1), cols], o[:])
+                nc.vector.tensor_tensor(res[:], sc[n][:] if n >= 2 else root[:], part[:], ALU.mult)
+                nc.sync.dma_start(out[P * h : P * (h + 1), cols], res[:])
+
+        for step in range(len(chunks) + 4):
+            for k in range(5):
+                if 0 <= step - k < len(chunks):
+                    stage(k, step - k)

from contextlib import ExitStack

import concourse.mybir as mybir
from concourse.masks import make_identity

K, T, S, H, V, Z = 512, 2048, 512, 512, 256, 512
FLOPS = 2 * (2 * K * H * S) + 2 * H * V * Z

F32 = mybir.dt.float32
BF16 = mybir.dt.bfloat16
I32 = mybir.dt.int32
U32 = mybir.dt.uint32
U16 = mybir.dt.uint16
U8 = mybir.dt.uint8
FP8X4 = mybir.dt.float8_e4m3fn_x4
ACT = mybir.ActivationFunctionType
ALU = mybir.AluOpType

P = 128
PACK = 4
CH = 256
SPLIT = 20
LAST = PACK - 1
TOP = P - 16


def tile_picked_yrxnlib_tan_p_kernel(
    tc, x_words, x_scales, w1, w2, e_words, e_scales, unit, nrm, offs, ra, rb, lib, out
):
    nc = tc.nc
    with ExitStack() as ctx:
        sb = ctx.enter_context(tc.tile_pool(name="sb", bufs=1))
        ps = ctx.enter_context(tc.psum_pool(name="ps", bufs=1))

        offs_t = sb.tile([P, S // 16], U16, name="offs_t")
        lib_t = sb.tile([P, Z // 16], U16, name="lib_t")
        ra_t = sb.tile([P, V // 16], U16, name="ra_t")
        rb_t = sb.tile([P, V // 16], U16, name="rb_t")
        xw = sb.tile([P, T], I32, name="xw")
        ew = sb.tile([P, T], I32, name="ew")
        xs = sb.tile([P, T], U8, name="xs")
        es = sb.tile([P, T], U8, name="es")
        eg_s = sb.tile([P, Z], U8, name="eg_s", align_bytes=64)
        w1_raw = [sb.tile([P, PACK, H // 2], F32, name=f"w1_raw{c}", tag=f"w1_raw{c}") for c in range(2)]
        w2_raw = [sb.tile([P, PACK, H // 2], F32, name=f"w2_raw{c}", tag=f"w2_raw{c}", align_bytes=64) for c in range(2)]
        nrm_t = sb.tile([P, T], F32, name="nrm_t")
        unit_t = sb.tile([P, PACK], F32, name="unit_t")

        nc.gpsimd.memset(xs[:].bitcast(I32), 0)
        nc.vector.memset(es[:TOP, :].bitcast(I32), 0)
        nc.vector.memset(nrm_t[: P - 1, :], 0.0)
        nc.vector.memset(eg_s[:].bitcast(I32), 0)

        nc.scalar.dma_start(es[TOP:, :].bitcast(I32), e_scales[0].bitcast(I32))
        nc.scalar.dma_start(nrm_t[P - 1 :, :], nrm[0:1, :])
        nc.gpsimd.dma_start(unit_t[:], unit.rearrange("(p t) o -> p (t o)", t=PACK))
        ident = sb.tile([P, P], F32, name="ident")
        make_identity(nc, ident[:])
        nc.sync.dma_start(offs_t[:], offs)
        nc.sync.dma_start(lib_t[:], lib)
        nc.sync.dma_start(xw[:], x_words[0].rearrange("p n r -> p (n r)").bitcast(I32))
        for q in range(4):
            nc.sync.dma_start(xs[32 * q : 32 * q + 4, :].bitcast(I32), x_scales[0, 4 * q : 4 * q + 4, :].bitcast(I32))
        for c in range(2):
            nc.sync.dma_start(w1_raw[c][:], w1.rearrange("(p j) c -> p j c", j=PACK)[:, :, 256 * c : 256 * (c + 1)])
        nc.sync.dma_start(rb_t[:], rb)
        for c in range(2):
            nc.sync.dma_start(w2_raw[c][:], w2.rearrange("(p j) c -> p j c", j=PACK)[:, :, 256 * c : 256 * (c + 1)])
        nc.sync.dma_start(ra_t[:], ra)
        nc.sync.dma_start(ew[:], e_words[0].rearrange("p n r -> p (n r)").bitcast(I32))

        eg_apart = sb.tile([P, Z], U8, name="eg_apart")
        nc.vector.tensor_copy(eg_apart[:], es[:].indirect(lib_t[:]))
        for q in range(4):
            nc.sync.dma_start(eg_s[32 * q : 32 * q + 4, :].bitcast(I32), eg_apart[TOP + 4 * q : TOP + 4 * q + 4, :].bitcast(I32))

        n_row = sb.tile([P, Z], F32, name="n_row")
        nc.scalar.activation(n_row[:], nrm_t[:].indirect(lib_t[:]), ACT.Copy, bias=0.3)
        turned = ps.tile([P, PACK, P], F32, name="turned", tag="bank4")
        for c in range(Z // P):
            nc.tensor.transpose(turned[:, c, :], n_row[:, P * c : P * (c + 1)], ident[:])
        n_col = sb.tile([P, Z // P], F32, name="n_col")
        nc.scalar.activation(n_col[:], turned[:, :, P - 1], ACT.Copy)
        ng = ps.tile([P, Z], F32, name="ng", tag="bank7")
        for c in range(Z // P):
            nc.tensor.transpose(ng[:, P * c : P * (c + 1)], n_col[:, c : c + 1].to_broadcast([P, P]), ident[:])

        gain = sb.tile([P, PACK], F32, name="gain")
        nc.gpsimd.tensor_scalar(gain[:, :LAST], unit_t[:, :LAST], 0.8, 0.0, ALU.mult, ALU.add)
        nc.gpsimd.tensor_scalar(gain[:, LAST:], unit_t[:, LAST:], 0.5, 0.0, ALU.mult, ALU.add)
        xg_s = sb.tile([P, S], U8, name="xg_s", align_bytes=64)

        def dealt(grouped):
            return grouped.rearrange("p (t m j) -> p m j t", t=PACK, j=PACK)

        def by_line(raw):
            return raw[:].rearrange("p j (m t) -> p m j t", t=PACK)

        def quantised(grouped, name):
            codes = sb.tile([P, H], U32, name=name + "_codes", align_bytes=64)
            scales = sb.tile([P, H], U8, name=name + "_scales", tag=name + "_scales", align_bytes=64)
            for h in range(2):
                nc.vector.quantize_mx(
                    out=codes[:, 256 * h : 256 * (h + 1)].bitcast(FP8X4),
                    scales=scales[:, 256 * h : 256 * (h + 1)],
                    in_=grouped[:, 1024 * h : 1024 * (h + 1)],
                )
            return codes, scales

        def first_product(codes, scales, t, bank):
            acc = ps.tile([P, S], F32, name=f"acc{bank}_{t}", tag=f"bank{bank}")
            cols = slice(P * t, P * (t + 1))
            nc.tensor.matmul_mx(
                out=acc[:], lhsT=codes[:, cols].bitcast(FP8X4), lhsT_scale=scales[:, cols],
                rhs=xg_w[:].bitcast(FP8X4), rhs_scale=xg_s[:], start=True, stop=True,
            )
            return acc

        w1_tile = sb.tile([P, PACK * H], BF16, name="w1_bf", align_bytes=64)
        w1_bf = w1_tile[:]
        w1_dst = dealt(w1_bf)
        xg_w = sb.tile([P, S], U32, name="xg_w", align_bytes=64)
        nc.vector.tensor_copy(xg_w[:], xw[:].bitcast(U32).indirect(offs_t[:]))
        nc.vector.tensor_copy(xg_s[:], xs[:].indirect(offs_t[:]))
        nc.scalar.activation(w1_dst[:, :64], by_line(w1_raw[0]), ACT.Copy)
        nc.scalar.activation(w1_dst[:, 64 : 64 + SPLIT], by_line(w1_raw[1])[:, :SPLIT], ACT.Copy)
        nc.vector.tensor_copy(w1_dst[:, 64 + SPLIT :], by_line(w1_raw[1])[:, SPLIT:])
        w1_codes, w1_scales = quantised(w1_bf, "w1")
        yh = []
        for t in range(PACK):
            y = first_product(w1_codes, w1_scales, t, t)
            yh_t = sb.tile([P, S], F32, name=f"yh{t}")
            nc.scalar.activation(yh_t[:], y[:], ACT.Copy, scale=gain[:, t : t + 1])
            yh.append(yh_t)

        w2_tile = sb.tile([P, PACK * H], BF16, name="w2_bf", tag="w2_bf", align_bytes=64)
        w2_bf = w2_tile[:]
        w2_dst = dealt(w2_bf)
        for c in range(2):
            nc.vector.tensor_copy(w2_dst[:, 64 * c : 64 * (c + 1)], by_line(w2_raw[c]))
        w2_codes, w2_scales = quantised(w2_bf, "w2")
        th = []
        for t in range(PACK):
            yl = first_product(w2_codes, w2_scales, t, (PACK + t) % 7)
            th_t = sb.tile([P, S], F32, name=f"th{t}", tag=f"th{t}", align_bytes=64)
            nc.scalar.activation(th_t[:], yl[:], ACT.Tanh, scale=-0.5)
            th.append(th_t)

        kept = sb.tile([P, PACK, V], F32, name="kept", tag="th1", align_bytes=64)
        joined = sb.tile([P, PACK, V], F32, name="joined", tag="w2_bf", align_bytes=64)
        for t in range(LAST):
            nc.vector.tensor_copy(joined[:, t, :], yh[t][:].indirect(rb_t[:]))
        nc.scalar.activation(joined[:, LAST, :], yh[LAST][:].indirect(rb_t[:]), ACT.Copy, scale=1.6)
        stay = []
        for t in range(PACK):
            stay_t = sb.tile([P, S], F32, name=f"stay{t}", tag=f"stay{t}")
            nc.vector.scalar_tensor_tensor(stay_t[:], th[t][:], 1.0, yh[t][:], ALU.add, ALU.mult)
            stay.append(stay_t)
        for t in range(LAST):
            nc.scalar.activation(kept[:, t, :], stay[t][:].indirect(ra_t[:]), ACT.Copy, scale=0.625)
        nc.scalar.activation(kept[:, LAST, :P], stay[LAST][:].indirect(ra_t[:, : P // 16]), ACT.Copy)
        nc.vector.tensor_copy(kept[:, LAST, P:], stay[LAST][:].indirect(ra_t[:, P // 16 :]))
        eg_w = sb.tile([P, Z], U32, name="eg_w", tag="th3", align_bytes=64)
        nc.vector.tensor_copy(eg_w[:], ew[:].bitcast(U32).indirect(lib_t[:]))

        warm = sb.tile([P, 1], F32, name="warm")
        nc.scalar.activation(warm[:], kept[:, LAST, 0:1], ACT.Abs_reciprocal_sqrt)
        h_codes = sb.tile([P, V], U32, name="h_codes", align_bytes=64)
        h_scales = sb.tile([P, V], U8, name="h_scales", align_bytes=64)
        kept_v = kept[:].rearrange("p t (c i) -> p c t i", i=4)
        joined_v = joined[:].rearrange("p t (c i) -> p c t i", i=4)
        for h in range(2):
            cs = slice(32 * h, 32 * (h + 1))
            hid = sb.tile([P, PACK * P], BF16, name=f"hid{h}", align_bytes=64)
            hid_v = hid[:].rearrange("p (c i t) -> p c t i", i=4, t=PACK)
            nc.vector.tensor_tensor(hid_v, kept_v[:, cs], joined_v[:, cs], ALU.add)
            vs = slice(P * h, P * (h + 1))
            nc.vector.quantize_mx(out=h_codes[:, vs].bitcast(FP8X4), scales=h_scales[:, vs], in_=hid[:])

        chunks = [(h, c) for h in range(2) for c in range(Z // CH)]
        sc = []
        for n, (h, c) in enumerate(chunks):
            vs, es_ = slice(P * h, P * (h + 1)), slice(CH * c, CH * (c + 1))
            acc = ps.tile([P, CH], F32, name=f"sc{n}", tag=f"bank{n + 1}")
            nc.tensor.matmul_mx(
                out=acc[:], lhsT=h_codes[:, vs].bitcast(FP8X4), lhsT_scale=h_scales[:, vs],
                rhs=eg_w[:, es_].bitcast(FP8X4), rhs_scale=eg_s[:, es_], start=True, stop=True,
            )
            sc.append(acc)
        work = {
            name: [sb.tile([P, CH], F32, name=f"{name}{n}") for n in range(len(chunks))]
            for name in ("mag", "den", "root", "part", "res")
        }

        def stage(k, n):
            h, c = chunks[n]
            cols = slice(CH * c, CH * (c + 1))
            mag, den, root, part, res = (work[name][n] for name in ("mag", "den", "root", "part", "res"))
            if k == 0:
                nc.scalar.activation(mag[:], sc[n][:], ACT.Abs)
            elif k == 1:
                nc.vector.tensor_tensor(den[:], ng[:, cols], mag[:], ALU.add)
            elif k == 2:
                nc.scalar.activation(root[:], den[:], ACT.Abs_reciprocal_sqrt)
            elif k == 3 and n >= 2:
                nc.scalar.activation(part[:], root[:], ACT.Square)
            elif k == 3:
                nc.vector.tensor_tensor(part[:], sc[n][:], root[:], ALU.mult)
            else:
                nc.vector.tensor_tensor(res[:], sc[n][:] if n >= 2 else root[:], part[:], ALU.mult)
                nc.sync.dma_start(out[P * h : P * (h + 1), cols], res[:])

        for step in range(len(chunks) + 4):
            for k in range(5):
                if 0 <= step - k < len(chunks):
                    stage(k, step - k)
